import numpy as np
import ml_dtypes


def mxq(x, axis, fmt="e4m3"):
    dtype, down = {"e4m3": (ml_dtypes.float8_e4m3fn, 7), "e5m2": (ml_dtypes.float8_e5m2, 14)}[fmt]
    v = np.moveaxis(np.asarray(x, np.float32).astype(ml_dtypes.bfloat16).astype(np.float64), axis, -1)
    blocks = v.reshape(v.shape[:-1] + (-1, 32))
    amax = np.abs(blocks).max(-1, keepdims=True)
    byte = np.maximum(np.where(amax > 0, np.frexp(amax)[1] - 1 + 127, 0) - down, 1)
    scale = np.exp2(byte - 127.0)
    codes = (blocks / scale).astype(np.float32).astype(dtype).astype(np.float64)
    return np.moveaxis((codes * scale).reshape(v.shape), -1, axis)


WIDE = False


def mx_kscale(k):
    if not WIDE:
        return np.ones(k)
    levels = np.array([10, -10, 5, -5, 0])
    if k % 512:
        return np.exp2(np.random.permutation(np.resize(levels, k // 32))).repeat(32)
    a = np.empty((k // 512, 16))
    for p in range(k // 512):
        a[p, :8] = np.random.permutation(np.resize(levels, 8))
        for g in range(8):
            far = levels[np.abs(levels - a[p, g]) >= 10]
            a[p, g + 8] = far[np.random.randint(len(far))]
    return np.exp2(a.ravel()).repeat(32)


def f64(x):
    return np.asarray(x).astype(np.float64)


def striped(idx):
    return np.tile(idx.reshape(-1, 16).T, (8, 1)).astype(np.uint16)


def unstriped(offs):
    return offs[:16].T.reshape(-1).astype(np.int64)


E2M1 = np.array([0.0, 0.5, 1.0, 1.5, 2.0, 3.0, 4.0, 6.0, -0.0, -0.5, -1.0, -1.5, -2.0, -3.0, -4.0, -6.0])


def pack_weight(w, fmt):
    k, n = w.shape
    w = f64(np.asarray(w, np.float32).astype(ml_dtypes.bfloat16)).reshape(k // 32, 32, n)
    amax = np.abs(w).max(1)
    if fmt == "e4m3":
        byte = np.frexp(amax)[1] - 1 + 127 - 7
    else:
        mant, ex = np.frexp(amax / 6.0)
        byte = np.where(mant > 0.5, ex, ex - 1) + 127
    byte = np.clip(np.where(amax > 0, byte, 1), 1, 254)
    scaled = (w * np.exp2(127.0 - byte)[:, None, :]).reshape(k, n).astype(np.float32)
    by_word = np.ascontiguousarray(scaled.reshape(k // 512, 128, 4, n).transpose(0, 1, 3, 2))
    if fmt == "e4m3":
        words = by_word.astype(ml_dtypes.float8_e4m3fn).view(np.uint8)
    else:
        c = by_word.astype(ml_dtypes.float4_e2m1fn).view(np.uint8) & 0xF
        words = (c[..., 0::2] | (c[..., 1::2] << 4)).reshape(k // 512, 128, 2 * n)
    return np.ascontiguousarray(words), np.ascontiguousarray(byte.astype(np.uint8).reshape(k // 512, 16, n))


def unpack_weight(words, scales, fmt):
    g, _, n = scales.shape
    words = np.ascontiguousarray(words).reshape(g, 128, n, -1)
    if fmt == "e4m3":
        vals = words.view(ml_dtypes.float8_e4m3fn).astype(np.float64)
    else:
        nib = np.empty((g, 128, n, 4), np.uint8)
        nib[..., 0::2] = words & 0xF
        nib[..., 1::2] = words >> 4
        vals = E2M1[nib]
    vals = vals * np.repeat(np.exp2(scales.astype(np.float64) - 127.0), 8, axis=1)[..., None]
    return vals.transpose(0, 1, 3, 2).reshape(g * 512, n)


def gelu(v):
    return 0.5 * v * (1.0 + np.tanh(np.sqrt(2.0 / np.pi) * (v + 0.044715 * v**3)))


def striped8(idx):
    return np.concatenate([v.reshape(-1, 16).T for v in idx]).astype(np.uint16)


def unstriped8(offs):
    return np.stack([offs[16 * g:16 * g + 16].T.reshape(-1) for g in range(8)]).astype(np.int64)


def runs(v, idx8):
    k = np.arange(v.shape[0])
    return v[k[:, None], idx8[k % 512 // 64]]


K, J, H, N, T, S, T2 = 1024, 512, 1024, 512, 2048, 512, 1024


def setup_inputs():
    n = np.random.standard_normal
    s = mx_kscale(K)[:, None]
    s2 = mx_kscale(J)[:, None]
    u = mx_kscale(H)[:, None]
    tab_words, tab_scales = pack_weight(n((K, T)) * s, "e4m3")
    tab2_words, tab2_scales = pack_weight(n((J, T)) * s2, "e4m3")
    w2_words, w2_scales = pack_weight(n((K, H)) / np.sqrt(K) / s * u.T, "e2m1")
    return {
        "tab_words": tab_words, "tab_scales": tab_scales,
        "offs": striped8(np.stack([np.random.permutation(T)[:S] for _ in range(8)])),
        "tab2_words": tab2_words, "tab2_scales": tab2_scales,
        "offs2": striped(np.random.permutation(T)[:S]),
        "w1": (n((K, H)) / np.sqrt(K) / s * u.T).astype(np.float32),
        "w2_words": w2_words, "w2_scales": w2_scales,
        "we": (1.5 * n((J, H)) / np.sqrt(J) / s2).astype(np.float32),
        "wj": (2.0 * n((H, N)) / np.sqrt(H) / u).astype(np.float32),
        "page1": n((N, T2)).astype(np.float32),
        "wgo": np.exp(0.3 * n((128, S))).astype(np.float32),
        "offs3": striped(np.random.permutation(T2)[:S]),
    }


def reference(tab_words, tab_scales, offs, tab2_words, tab2_scales, offs2, w1, w2_words, w2_scales, we, wj, page1, wgo, offs3):
    v = runs(unpack_weight(tab_words, tab_scales, "e4m3"), unstriped8(offs))
    v2 = unpack_weight(tab2_words, tab2_scales, "e4m3")[:, unstriped(offs2)]
    b1 = mxq(f64(w1), 0, "e4m3").T @ v
    b2 = unpack_weight(w2_words, w2_scales, "e2m1").T @ v
    e = mxq(f64(we), 0, "e4m3").T @ v2
    h = np.minimum(b1, b2) / (1.0 + np.abs(e))
    y = mxq(f64(wj), 0, "e4m3").T @ mxq(h, 0, "e4m3")
    out = f64(page1).copy()
    out[:, unstriped(offs3)] = np.tile(f64(wgo), (N // 128, 1)) * y
    return out

@@ -1,0 +1,336 @@
+from contextlib import ExitStack
+
+import concourse.mybir as mybir
+
+K, J, H, N, T, S, T2 = 1024, 512, 1024, 512, 2048, 512, 1024
+FLOPS = 2 * S * (2 * K * H + J * H + H * N)
+
+F32 = mybir.dt.float32
+BF16 = mybir.dt.bfloat16
+I32 = mybir.dt.int32
+U32 = mybir.dt.uint32
+U16 = mybir.dt.uint16
+U8 = mybir.dt.uint8
+FP8X4 = mybir.dt.float8_e4m3fn_x4
+FP4X4 = mybir.dt.float4_e2m1fn_x4
+ACT = mybir.ActivationFunctionType
+ALU = mybir.AluOpType
+
+P = 128
+C = 128
+CHUNKS = S // C
+
+
+def tile_list_etched_weld_contrast_kernel(
+    tc, tab_words, tab_scales, offs, tab2_words, tab2_scales, offs2, w1, w2_words, w2_scales, we, wj, page1, wgo, offs3, out
+):
+    nc = tc.nc
+    with ExitStack() as ctx:
+        keep = ctx.enter_context(tc.tile_pool(name="keep", bufs=1))
+        ring = ctx.enter_context(tc.tile_pool(name="ring", bufs=1))
+        psum = ctx.enter_context(tc.psum_pool(name="psum", bufs=8))
+
+        def kept(name, shape, dtype):
+            return keep.tile(shape, dtype, name=name, align_bytes=64)
+
+        def ringed(tag, shape, dtype, bufs):
+            return ring.tile(shape, dtype, name=tag, tag=tag, bufs=bufs, align_bytes=64)
+
+        list1 = kept("list1", [P, S // 16], U16)
+        list2 = kept("list2", [P, S // 16], U16)
+        list3 = kept("list3", [P, S // 16], U16)
+        tab_sc = kept("tab_sc", [P, T], U8)
+        tab2_sc = ringed("slot_d", [P, T], U8, 1)
+        w2_sc_raw = kept("w2_sc_raw", [P, 2, H], U8)
+        v_plane = kept("v_plane", [P, 2, S], U8)
+        nc.gpsimd.memset(tab_sc[:].bitcast(I32), 0)
+        nc.vector.memset(tab2_sc[:].bitcast(I32), 0)
+        for zeroed in (w2_sc_raw, v_plane):
+            nc.vector.memset(zeroed[:].rearrange("p a n -> p (a n)").bitcast(I32), 0)
+
+        for a in range(2):
+            nc.gpsimd.dma_start(out=tab_sc[a:P:8, :].bitcast(I32), in_=tab_scales[a].bitcast(I32))
+        for d in range(4):
+            nc.gpsimd.dma_start(
+                out=w2_sc_raw[32 * d : 32 * d + 4].bitcast(I32),
+                in_=w2_scales[:, 4 * d : 4 * d + 4, :].rearrange("a q n -> q a n").bitcast(I32),
+            )
+
+        def load_weight(w, a, b, slot):
+            raw = ringed(slot, [P, 4, 512], F32, 1)
+            nc.sync.dma_start(out=raw[:], in_=w[512 * a : 512 * (a + 1), 512 * b : 512 * (b + 1)].rearrange("(p j) c -> p j c", j=4))
+            return raw
+
+        def load_words(slot, words):
+            win = ringed(slot, [P, T], U32, 1)
+            nc.sync.dma_start(out=win[:].bitcast(I32), in_=words.rearrange("p t i -> p (t i)").bitcast(I32))
+            return win
+
+        def gather(name, win, lst, dtype):
+            got = kept(name, [P, S], dtype)
+            nc.vector.tensor_copy(got[:], win[:].indirect(lst[:]))
+            return got
+
+        def weave(engine, dst, src):
+            if engine == "v":
+                nc.vector.tensor_copy(out=dst, in_=src)
+            else:
+                nc.scalar.copy(out=dst, in_=src)
+
+        def quantise_weight(name, raw, engines):
+            codes = ringed(name + "_codes", [P, 512], U32, 1)
+            scales = kept(name + "_scales", [P, 512], U8)
+            src = raw[:].rearrange("p j (i t u) -> p t i j u", t=4, u=4)
+            halves = []
+            for h in range(2):
+                half = ringed("half", [P, 2, P, 4], BF16, 4)
+                weave(engines[h], half[:].rearrange("p t (i u) j -> p t i j u", u=4), src[:, 2 * h : 2 * h + 2])
+                halves.append(half)
+            for h in range(2):
+                cols = slice(256 * h, 256 * (h + 1))
+                nc.vector.quantize_mx(
+                    out=codes[:, cols].bitcast(FP8X4), scales=scales[:, cols], in_=halves[h][:].rearrange("p t m j -> p (t m j)")
+                )
+            return codes, scales
+
+        def first_stage(passes, c):
+            bank = psum.tile([P, 4, C], F32, name="bank", tag="bank")
+            cols = slice(C * c, C * (c + 1))
+            for t in range(4):
+                for n, (lhs, lhs_scale, rhs, rhs_scale) in enumerate(passes):
+                    nc.tensor.matmul_mx(
+                        out=bank[:, t, :],
+                        lhsT=lhs(t),
+                        lhsT_scale=lhs_scale(t),
+                        rhs=rhs[:, cols].bitcast(FP8X4),
+                        rhs_scale=rhs_scale[:, cols],
+                        start=(n == 0),
+                        stop=(n == len(passes) - 1),
+                    )
+            return bank[:].rearrange("p t j -> p j t")
+
+        def woven(tile):
+            return tile[:].rearrange("p (j t) -> p j t", t=4)
+
+        def fp8_pass(q, rhs, rhs_scale):
+            codes, scales = q
+            return (lambda t: codes[:, P * t : P * (t + 1)].bitcast(FP8X4), lambda t: scales[:, P * t : P * (t + 1)], rhs, rhs_scale)
+
+        def damping_tiles():
+            return [ringed(tag, [P, 4 * S], F32, 1) for tag in ("size", "root", "damp")]
+
+        def span(tile, c, count=1):
+            return tile[:, 4 * C * c : 4 * C * (c + count)]
+
+        def take_size(we_q, size, c):
+            e = first_stage([fp8_pass(we_q, v2_words, v2_plane)], c)
+            nc.scalar.activation(out=span(size, c).rearrange("p (j t) -> p j t", t=4), in_=e, func=ACT.Abs)
+
+        def take_root(size, root, c, count=1):
+            nc.scalar.activation(out=span(root, c, count), in_=span(size, c, count), func=ACT.Abs_reciprocal_sqrt, bias=1.0)
+
+        def take_square(root, damp, c, count=1):
+            nc.scalar.activation(out=span(damp, c, count), in_=span(root, c, count), func=ACT.Square)
+
+        def second_response(b, c):
+            passes = [
+                (
+                    lambda t, a=a: w2_dealt[:, 8 * a + 4 * b + t, :].bitcast(FP4X4),
+                    lambda t, a=a: w2_sc[:, 8 * a + 4 * b + t, :],
+                    v_words[a],
+                    v_plane[:, a, :],
+                )
+                for a in range(2)
+            ]
+            b2 = first_stage(passes, c)
+            held = ringed("held", [P, 4 * C], F32, 6)
+            nc.scalar.copy(out=woven(held), in_=b2)
+            return held
+
+        def smaller(w1_q, held, c):
+            b1 = first_stage([fp8_pass(w1_q[a], v_words[a], v_plane[:, a, :]) for a in range(2)], c)
+            least = ringed("least", [P, 4 * C], F32, 4)
+            nc.vector.tensor_tensor(out=woven(least), in0=b1, in1=woven(held), op=ALU.min)
+            return least
+
+        h_codes = [kept("h_codes%d" % b, [P, S], U32) for b in range(2)]
+        h_scales = [kept("h_scales%d" % b, [P, S], U8) for b in range(2)]
+
+        def damped(least, damp):
+            h = ringed("h", [P, 4 * C], BF16, 2)
+            nc.vector.tensor_tensor(out=h[:], in0=least[:], in1=damp, op=ALU.mult)
+            return h
+
+        def quantise_h(h, b, c):
+            cols = slice(C * c, C * (c + 1))
+            nc.vector.quantize_mx(out=h_codes[b][:, cols].bitcast(FP8X4), scales=h_scales[b][:, cols], in_=h[:])
+
+        def move_scales(a, d):
+            nc.sync.dma_start(
+                out=v_plane[32 * d : 32 * d + 4, a, :].bitcast(I32), in_=v_sc[32 * d + a : 32 * (d + 1) : 8, :].bitcast(I32)
+            )
+
+        nc.sync.dma_start(list2[:], offs2)
+        nc.sync.dma_start(list1[:], offs)
+        we0_raw = load_weight(we, 0, 0, "slot_a")
+        for d in range(4):
+            nc.scalar.dma_start(out=tab2_sc[32 * d : 32 * d + 4, :].bitcast(I32), in_=tab2_scales[0, 4 * d : 4 * d + 4, :].bitcast(I32))
+        tab2_win = load_words("slot_b", tab2_words[0])
+        w2_raw = ringed("slot_c", [P, 2, 512], I32, 1)
+        nc.sync.dma_start(out=w2_raw[:], in_=w2_words.rearrange("a p n -> p a n").bitcast(I32))
+        nc.sync.dma_start(list3[:], offs3)
+
+        v2_plane = gather("v2_plane", tab2_sc, list2, U8)
+        v_sc = gather("v_sc", tab_sc, list1, U8)
+        tab_win0 = load_words("slot_d", tab_words[0])
+        we0_q = quantise_weight("we0", we0_raw, "ss")
+        v2_words = gather("v2_words", tab2_win, list2, U32)
+
+        for d in range(2):
+            move_scales(0, d)
+        w1_raw00 = load_weight(w1, 0, 0, "slot_a")
+        for d in range(2, 4):
+            move_scales(0, d)
+        for d in range(4):
+            move_scales(1, d)
+        tab_win1 = load_words("slot_b", tab_words[1])
+
+        size, root, damp = damping_tiles()
+        for c in range(CHUNKS):
+            take_size(we0_q, size, c)
+        for c in range(0, CHUNKS, 2):
+            take_root(size, root, c, 2)
+        for c in range(0, CHUNKS, 2):
+            take_square(root, damp, c, 2)
+
+        w2_sc = kept("w2_sc", [P, 16, P], U8)
+        nc.vector.tensor_copy(
+            out=w2_sc[:].bitcast(I32).rearrange("p (g t) i -> p g t i", t=4),
+            in_=w2_sc_raw[:].bitcast(I32).rearrange("p a (b i t) -> p (a b) t i", b=2, t=4),
+        )
+        w2_dealt = kept("w2_dealt", [P, 16, 2 * P], U8)
+        nc.vector.tensor_copy(
+            out=w2_dealt[:].bitcast(I32).rearrange("p (g t) (i w) -> p g t i w", t=4, w=2),
+            in_=w2_raw[:].rearrange("p a (b i t w) -> p (a b) t i w", b=2, t=4, w=2),
+        )
+        w1_raw10 = load_weight(w1, 1, 0, "slot_c")
+        v_words = [gather("v_words0", tab_win0, list1, U32)]
+        w1_raw01 = load_weight(w1, 0, 1, "slot_d")
+        w1_q0 = [quantise_weight("w1_00", w1_raw00, "vv")]
+        w1_raw11 = load_weight(w1, 1, 1, "slot_a")
+        v_words.append(gather("v_words1", tab_win1, list1, U32))
+        we1_raw = load_weight(we, 0, 1, "slot_b")
+        w1_q0.append(quantise_weight("w1_10", w1_raw10, "vs"))
+        held0 = [second_response(0, c) for c in range(CHUNKS)]
+
+        w1_q1 = []
+        for c in range(CHUNKS):
+            least = smaller(w1_q0, held0[c], c)
+            if c == 1:
+                w1_q1.append(quantise_weight("w1_01", w1_raw01, "ss"))
+            quantise_h(damped(least, span(damp, c)), 0, c)
+
+        w1_q1.append(quantise_weight("w1_11", w1_raw11, "vs"))
+        held1 = [second_response(1, c) for c in range(CHUNKS)]
+        we1_q = quantise_weight("we1", we1_raw, "vv")
+
+        wj_raw = {}
+
+        def load_wj(g, slot):
+            wj_raw[g] = ringed(slot, [P, 2, 4, 256], F32, 1)
+            for b in range(2):
+                rows = wj[512 * b : 512 * (b + 1), 256 * g : 256 * (g + 1)].rearrange("(i t u) n -> u i t n", t=4, u=4)
+                for u in range(4):
+                    nc.sync.dma_start(out=wj_raw[g][u:P:4, b], in_=rows[u])
+
+        pages = {}
+
+        def load_page(n, slot):
+            pages[n] = ringed(slot, [P, T2], F32, 1)
+            nc.sync.dma_start(out=pages[n][:], in_=page1[P * n : P * (n + 1), :])
+
+        load_wj(0, "slot_c")
+        gain = ringed("half", [P, S], F32, 4)
+        nc.sync.dma_start(out=gain[:], in_=wgo)
+        load_page(0, "slot_d")
+        load_page(1, "slot_a")
+        load_wj(1, "slot_b")
+
+        wj_q = {}
+
+        def quantise_wj(n, engine):
+            codes = kept("wj_codes%d" % n, [P, 2, P], U32)
+            scales = kept("wj_scales%d" % n, [P, 2, P], U8)
+            both = ringed("both", [P, 2, P, 4], BF16, 2)
+            src = wj_raw[n // 2][:, :, :, P * (n % 2) : P * (n % 2 + 1)]
+            weave(engine, both[:].rearrange("p b (i u) t -> p b i t u", u=4), src.rearrange("p b t (i u) -> p b i t u", u=4))
+            nc.vector.quantize_mx(
+                out=codes[:].rearrange("p b m -> p (b m)").bitcast(FP8X4),
+                scales=scales[:].rearrange("p b m -> p (b m)"),
+                in_=both[:].rearrange("p b m t -> p (b m t)"),
+            )
+            wj_q[n] = (codes, scales)
+
+        def contrast(n, c, count):
+            cols = slice(C * c, C * (c + count))
+            bank = psum.tile([P, C * count], F32, name="bank", tag="bank")
+            codes, scales = wj_q[n]
+            for b in range(2):
+                nc.tensor.matmul_mx(
+                    out=bank[:],
+                    lhsT=codes[:, b, :].bitcast(FP8X4),
+                    lhsT_scale=scales[:, b, :],
+                    rhs=h_codes[b][:, cols].bitcast(FP8X4),
+                    rhs_scale=h_scales[b][:, cols],
+                    start=(b == 0),
+                    stop=(b == 1),
+                )
+            y = ringed("y", [P, C * count], F32, 4)
+            nc.scalar.copy(out=y[:], in_=bank[:])
+            return y
+
+        def put(y, n, c, count):
+            cols = slice(C * c, C * (c + count))
+            entries = list3[:, C // 16 * c : C // 16 * (c + count)]
+            nc.vector.tensor_tensor(out=pages[n][:].indirect(entries), in0=y[:], in1=gain[:, cols], op=ALU.mult)
+
+        def finish_h(c):
+            quantise_h(damped(least1[c], span(damp, c)), 1, c)
+
+        def store(n):
+            nc.sync.dma_start(out=out[P * n : P * (n + 1), :], in_=pages[n][:])
+
+        size, root, damp = damping_tiles()
+        take_size(we1_q, size, 0)
+        take_size(we1_q, size, 1)
+        take_root(size, root, 0)
+        take_size(we1_q, size, 2)
+        take_square(root, damp, 0)
+        least1 = [smaller(w1_q1, held1[c], c) for c in range(CHUNKS)]
+        quantise_wj(0, "v")
+        finish_h(0)
+        take_root(size, root, 1)
+        take_size(we1_q, size, 3)
+        take_square(root, damp, 1)
+        y = contrast(0, 0, 1)
+        for c in range(1, CHUNKS):
+            finish_h(c)
+            put(y, 0, c - 1, 1)
+            if c + 1 < CHUNKS:
+                take_root(size, root, c + 1)
+            y = contrast(0, c, 1)
+            if c + 1 < CHUNKS:
+                take_square(root, damp, c + 1)
+        quantise_wj(1, "s")
+        load_page(2, "slot_c")
+        load_page(3, "w1_11_codes")
+        put(y, 0, CHUNKS - 1, 1)
+        store(0)
+        y = contrast(1, 0, 4)
+        for n in range(1, 4):
+            if n < 3:
+                quantise_wj(n + 1, "s")
+            put(y, n, 0, 4)
+            store(n)
+            if n < 3:
+                y = contrast(n + 1, 0, 4)

@@ -28,6 +28,7 @@ def tile_list_etched_weld_contrast_kernel(
     with ExitStack() as ctx:
         keep = ctx.enter_context(tc.tile_pool(name="keep", bufs=1))
         ring = ctx.enter_context(tc.tile_pool(name="ring", bufs=1))
+        lap = ctx.enter_context(tc.tile_pool(name="lap", bufs=1))
         psum = ctx.enter_context(tc.psum_pool(name="psum", bufs=8))
 
         def kept(name, shape, dtype):
@@ -36,38 +37,43 @@ def tile_list_etched_weld_contrast_kernel(
         def ringed(tag, shape, dtype, bufs):
             return ring.tile(shape, dtype, name=tag, tag=tag, bufs=bufs, align_bytes=64)
 
+        def placed(name, shape, dtype, place):
+            if isinstance(place, str):
+                return ringed(place, shape, dtype, 1)
+            return lap.tile(shape, dtype, name=name, tag=name, offset=1024 * place, align_bytes=64)
+
         list1 = kept("list1", [P, S // 16], U16)
         list2 = kept("list2", [P, S // 16], U16)
         list3 = kept("list3", [P, S // 16], U16)
-        tab_sc = kept("tab_sc", [P, T], U8)
-        tab2_sc = ringed("slot_d", [P, T], U8, 1)
+        tab_sc = [placed("tab_sc%d" % a, [P, T], U8, 8 + 2 * a) for a in range(2)]
+        tab2_sc = placed("tab2_sc", [P, T], U8, 24)
+        tab2_rows = ringed("slot_c", [P, T // 4], I32, 1)
         w2_sc_raw = kept("w2_sc_raw", [P, 2, H], U8)
         v_plane = kept("v_plane", [P, 2, S], U8)
-        nc.gpsimd.memset(tab_sc[:].bitcast(I32), 0)
         nc.vector.memset(tab2_sc[:].bitcast(I32), 0)
+        nc.gpsimd.memset(tab_sc[0][:].bitcast(I32), 0)
+        nc.vector.memset(tab_sc[1][:].bitcast(I32), 0)
         for zeroed in (w2_sc_raw, v_plane):
             nc.vector.memset(zeroed[:].rearrange("p a n -> p (a n)").bitcast(I32), 0)
 
-        for a in range(2):
-            nc.gpsimd.dma_start(out=tab_sc[a:P:8, :].bitcast(I32), in_=tab_scales[a].bitcast(I32))
         for d in range(4):
             nc.gpsimd.dma_start(
                 out=w2_sc_raw[32 * d : 32 * d + 4].bitcast(I32),
                 in_=w2_scales[:, 4 * d : 4 * d + 4, :].rearrange("a q n -> q a n").bitcast(I32),
             )
 
-        def load_weight(w, a, b, slot):
-            raw = ringed(slot, [P, 4, 512], F32, 1)
+        def load_weight(name, w, a, b, place):
+            raw = placed(name, [P, 4, 512], F32, place)
             nc.sync.dma_start(out=raw[:], in_=w[512 * a : 512 * (a + 1), 512 * b : 512 * (b + 1)].rearrange("(p j) c -> p j c", j=4))
             return raw
 
-        def load_words(slot, words):
-            win = ringed(slot, [P, T], U32, 1)
+        def load_words(name, words, place):
+            win = placed(name, [P, T], U32, place)
             nc.sync.dma_start(out=win[:].bitcast(I32), in_=words.rearrange("p t i -> p (t i)").bitcast(I32))
             return win
 
-        def gather(name, win, lst, dtype):
-            got = kept(name, [P, S], dtype)
+        def gather(name, win, lst, dtype, place):
+            got = placed(name, [P, S], dtype, place)
             nc.vector.tensor_copy(got[:], win[:].indirect(lst[:]))
             return got
 
@@ -77,40 +83,45 @@ def tile_list_etched_weld_contrast_kernel(
             else:
                 nc.scalar.copy(out=dst, in_=src)
 
-        def quantise_weight(name, raw, engines):
-            codes = ringed(name + "_codes", [P, 512], U32, 1)
+        def quantise_weight(name, raw, engines, places, codes_place):
+            codes = placed(name + "_codes", [P, 512], U32, codes_place)
             scales = kept(name + "_scales", [P, 512], U8)
             src = raw[:].rearrange("p j (i t u) -> p t i j u", t=4, u=4)
-            halves = []
-            for h in range(2):
-                half = ringed("half", [P, 2, P, 4], BF16, 4)
-                weave(engines[h], half[:].rearrange("p t (i u) j -> p t i j u", u=4), src[:, 2 * h : 2 * h + 2])
-                halves.append(half)
-            for h in range(2):
-                cols = slice(256 * h, 256 * (h + 1))
+            share = 4 // len(engines)
+            parts = []
+            for h, engine in enumerate(engines):
+                part = placed(name + "_woven%d" % h, [P, share, P, 4], BF16, places[h])
+                weave(engine, part[:].rearrange("p t (i u) j -> p t i j u", u=4), src[:, share * h : share * (h + 1)])
+                parts.append(part)
+            for h, part in enumerate(parts):
+                cols = slice(P * share * h, P * share * (h + 1))
                 nc.vector.quantize_mx(
-                    out=codes[:, cols].bitcast(FP8X4), scales=scales[:, cols], in_=halves[h][:].rearrange("p t m j -> p (t m j)")
+                    out=codes[:, cols].bitcast(FP8X4), scales=scales[:, cols], in_=part[:].rearrange("p t m j -> p (t m j)")
                 )
             return codes, scales
 
-        def first_stage(passes, c):
-            bank = psum.tile([P, 4, C], F32, name="bank", tag="bank")
+        def new_bank():
+            return psum.tile([P, 4, C], F32, name="bank", tag="bank")
+
+        def add_pass(bank, operands, c, first, last):
+            lhs, lhs_scale, rhs, rhs_scale = operands
             cols = slice(C * c, C * (c + 1))
             for t in range(4):
-                for n, (lhs, lhs_scale, rhs, rhs_scale) in enumerate(passes):
-                    nc.tensor.matmul_mx(
-                        out=bank[:, t, :],
-                        lhsT=lhs(t),
-                        lhsT_scale=lhs_scale(t),
-                        rhs=rhs[:, cols].bitcast(FP8X4),
-                        rhs_scale=rhs_scale[:, cols],
-                        start=(n == 0),
-                        stop=(n == len(passes) - 1),
-                    )
+                nc.tensor.matmul_mx(
+                    out=bank[:, t, :],
+                    lhsT=lhs(t),
+                    lhsT_scale=lhs_scale(t),
+                    rhs=rhs[:, cols].bitcast(FP8X4),
+                    rhs_scale=rhs_scale[:, cols],
+                    start=(first and t == 0),
+                    stop=(last and t == 3),
+                )
+
+        def stepped(bank):
             return bank[:].rearrange("p t j -> p j t")
 
-        def woven(tile):
-            return tile[:].rearrange("p (j t) -> p j t", t=4)
+        def woven(ap):
+            return ap.rearrange("p (j t) -> p j t", t=4)
 
         def fp8_pass(q, rhs, rhs_scale):
             codes, scales = q
@@ -123,8 +134,9 @@ def tile_list_etched_weld_contrast_kernel(
             return tile[:, 4 * C * c : 4 * C * (c + count)]
 
         def take_size(we_q, size, c):
-            e = first_stage([fp8_pass(we_q, v2_words, v2_plane)], c)
-            nc.scalar.activation(out=span(size, c).rearrange("p (j t) -> p j t", t=4), in_=e, func=ACT.Abs)
+            bank = new_bank()
+            add_pass(bank, fp8_pass(we_q, v2_words, v2_plane), c, True, True)
+            nc.scalar.activation(out=woven(span(size, c)), in_=stepped(bank), func=ACT.Abs)
 
         def take_root(size, root, c, count=1):
             nc.scalar.activation(out=span(root, c, count), in_=span(size, c, count), func=ACT.Abs_reciprocal_sqrt, bias=1.0)
@@ -132,68 +144,62 @@ def tile_list_etched_weld_contrast_kernel(
         def take_square(root, damp, c, count=1):
             nc.scalar.activation(out=span(damp, c, count), in_=span(root, c, count), func=ACT.Square)
 
-        def second_response(b, c):
-            passes = [
-                (
-                    lambda t, a=a: w2_dealt[:, 8 * a + 4 * b + t, :].bitcast(FP4X4),
-                    lambda t, a=a: w2_sc[:, 8 * a + 4 * b + t, :],
-                    v_words[a],
-                    v_plane[:, a, :],
-                )
-                for a in range(2)
-            ]
-            b2 = first_stage(passes, c)
-            held = ringed("held", [P, 4 * C], F32, 6)
-            nc.scalar.copy(out=woven(held), in_=b2)
+        def fp4_pass(a, b):
+            return (
+                lambda t: w2_dealt[:, 8 * a + 4 * b + t, :].bitcast(FP4X4),
+                lambda t: w2_sc[:, 8 * a + 4 * b + t, :],
+                v_words[a],
+                v_plane[:, a, :],
+            )
+
+        def hold(bank, tag):
+            held = ringed(tag, [P, 4 * C], F32, 1)
+            nc.scalar.copy(out=woven(held[:]), in_=stepped(bank))
             return held
 
-        def smaller(w1_q, held, c):
-            b1 = first_stage([fp8_pass(w1_q[a], v_words[a], v_plane[:, a, :]) for a in range(2)], c)
-            least = ringed("least", [P, 4 * C], F32, 4)
-            nc.vector.tensor_tensor(out=woven(least), in0=b1, in1=woven(held), op=ALU.min)
-            return least
+        def smaller(bank, held, least):
+            nc.vector.tensor_tensor(out=woven(least), in0=stepped(bank), in1=woven(held[:]), op=ALU.min)
 
         h_codes = [kept("h_codes%d" % b, [P, S], U32) for b in range(2)]
         h_scales = [kept("h_scales%d" % b, [P, S], U8) for b in range(2)]
 
-        def damped(least, damp):
-            h = ringed("h", [P, 4 * C], BF16, 2)
-            nc.vector.tensor_tensor(out=h[:], in0=least[:], in1=damp, op=ALU.mult)
+        def damped(least, damp, c, count, tag):
+            h = ringed(tag, [P, 4 * C * count], BF16, 1)
+            nc.vector.tensor_tensor(out=h[:], in0=least, in1=span(damp, c, count), op=ALU.mult)
             return h
 
-        def quantise_h(h, b, c):
-            cols = slice(C * c, C * (c + 1))
+        def quantise_h(h, b, c, count=1):
+            cols = slice(C * c, C * (c + count))
             nc.vector.quantize_mx(out=h_codes[b][:, cols].bitcast(FP8X4), scales=h_scales[b][:, cols], in_=h[:])
 
-        def move_scales(a, d):
-            nc.sync.dma_start(
-                out=v_plane[32 * d : 32 * d + 4, a, :].bitcast(I32), in_=v_sc[32 * d + a : 32 * (d + 1) : 8, :].bitcast(I32)
-            )
-
         nc.sync.dma_start(list2[:], offs2)
-        nc.sync.dma_start(list1[:], offs)
-        we0_raw = load_weight(we, 0, 0, "slot_a")
         for d in range(4):
-            nc.scalar.dma_start(out=tab2_sc[32 * d : 32 * d + 4, :].bitcast(I32), in_=tab2_scales[0, 4 * d : 4 * d + 4, :].bitcast(I32))
-        tab2_win = load_words("slot_b", tab2_words[0])
-        w2_raw = ringed("slot_c", [P, 2, 512], I32, 1)
-        nc.sync.dma_start(out=w2_raw[:], in_=w2_words.rearrange("a p n -> p a n").bitcast(I32))
+            nc.sync.dma_start(out=tab2_rows[32 * d : 32 * d + 4, :], in_=tab2_scales[0, 4 * d : 4 * d + 4, :].bitcast(I32))
+        we0_raw = load_weight("we0", we, 0, 0, "slot_a")
+        tab2_win = load_words("tab2_win", tab2_words[0], "slot_b")
+        nc.sync.dma_start(list1[:], offs)
+        for a in range(2):
+            nc.sync.dma_start(out=tab_sc[a][0:P:8, :].bitcast(I32), in_=tab_scales[a].bitcast(I32))
         nc.sync.dma_start(list3[:], offs3)
 
-        v2_plane = gather("v2_plane", tab2_sc, list2, U8)
-        v_sc = gather("v_sc", tab_sc, list1, U8)
-        tab_win0 = load_words("slot_d", tab_words[0])
-        we0_q = quantise_weight("we0", we0_raw, "ss")
-        v2_words = gather("v2_words", tab2_win, list2, U32)
-
-        for d in range(2):
-            move_scales(0, d)
-        w1_raw00 = load_weight(w1, 0, 0, "slot_a")
-        for d in range(2, 4):
-            move_scales(0, d)
         for d in range(4):
-            move_scales(1, d)
-        tab_win1 = load_words("slot_b", tab_words[1])
+            nc.vector.tensor_copy(out=tab2_sc[32 * d : 32 * d + 4, :].bitcast(I32), in_=tab2_rows[32 * d : 32 * d + 4, :])
+        w2_raw = ringed("slot_c", [P, 2, 512], I32, 1)
+        nc.sync.dma_start(out=w2_raw[:], in_=w2_words.rearrange("a p n -> p a n").bitcast(I32))
+        v2_plane = gather("v2_plane", tab2_sc, list2, U8, "v2_plane")
+        tab_win0 = load_words("tab_win0", tab_words[0], 22)
+        we0_q = quantise_weight("we0", we0_raw, "vs", ("woven0", "early"), "we0_codes")
+        v2_words = gather("v2_words", tab2_win, list2, U32, "v2_words")
+        w1_raw00 = load_weight("w1_00", w1, 0, 0, "slot_a")
+        v_sc = ringed("early", [P, 2, S], U8, 1)
+        for a in range(2):
+            nc.vector.tensor_copy(v_sc[:, a, :], tab_sc[a][:].indirect(list1[:]))
+        for d in range(4):
+            nc.sync.dma_start(
+                out=v_plane[32 * d : 32 * d + 4].rearrange("p a n -> p (a n)").bitcast(I32),
+                in_=v_sc[32 * d : 32 * (d + 1) : 8].rearrange("p a n -> p (a n)").bitcast(I32),
+            )
+        tab_win1 = load_words("tab_win1", tab_words[1], 11)
 
         size, root, damp = damping_tiles()
         for c in range(CHUNKS):
@@ -203,41 +209,60 @@ def tile_list_etched_weld_contrast_kernel(
         for c in range(0, CHUNKS, 2):
             take_square(root, damp, c, 2)
 
-        w2_sc = kept("w2_sc", [P, 16, P], U8)
-        nc.vector.tensor_copy(
-            out=w2_sc[:].bitcast(I32).rearrange("p (g t) i -> p g t i", t=4),
-            in_=w2_sc_raw[:].bitcast(I32).rearrange("p a (b i t) -> p (a b) t i", b=2, t=4),
-        )
-        w2_dealt = kept("w2_dealt", [P, 16, 2 * P], U8)
+        w2_dealt = placed("w2_dealt", [P, 16, 2 * P], U8, 5)
         nc.vector.tensor_copy(
             out=w2_dealt[:].bitcast(I32).rearrange("p (g t) (i w) -> p g t i w", t=4, w=2),
             in_=w2_raw[:].rearrange("p a (b i t w) -> p (a b) t i w", b=2, t=4, w=2),
         )
-        w1_raw10 = load_weight(w1, 1, 0, "slot_c")
-        v_words = [gather("v_words0", tab_win0, list1, U32)]
-        w1_raw01 = load_weight(w1, 0, 1, "slot_d")
-        w1_q0 = [quantise_weight("w1_00", w1_raw00, "vv")]
-        w1_raw11 = load_weight(w1, 1, 1, "slot_a")
-        v_words.append(gather("v_words1", tab_win1, list1, U32))
-        we1_raw = load_weight(we, 0, 1, "slot_b")
-        w1_q0.append(quantise_weight("w1_10", w1_raw10, "vs"))
-        held0 = [second_response(0, c) for c in range(CHUNKS)]
-
-        w1_q1 = []
+        w2_sc = ringed("slot_c", [P, 16, P], U8, 1)
+        nc.vector.tensor_copy(
+            out=w2_sc[:].bitcast(I32).rearrange("p (g t) i -> p g t i", t=4),
+            in_=w2_sc_raw[:].bitcast(I32).rearrange("p a (b i t) -> p (a b) t i", b=2, t=4),
+        )
+        v_words = [gather("v_words0", tab_win0, list1, U32, 9)]
+        w1_raw10 = load_weight("w1_10", w1, 1, 0, 24)
+        second = [new_bank() for c in range(CHUNKS)]
         for c in range(CHUNKS):
-            least = smaller(w1_q0, held0[c], c)
-            if c == 1:
-                w1_q1.append(quantise_weight("w1_01", w1_raw01, "ss"))
-            quantise_h(damped(least, span(damp, c)), 0, c)
+            add_pass(second[c], fp4_pass(0, 0), c, True, False)
+        w1_q00 = quantise_weight("w1_00", w1_raw00, "v", (20,), "w1_00_codes")
+        w1_raw01 = load_weight("w1_01", w1, 0, 1, "slot_a")
+        first = [new_bank() for c in range(CHUNKS)]
+        for c in range(CHUNKS):
+            add_pass(first[c], fp8_pass(w1_q00, v_words[0], v_plane[:, 0, :]), c, True, False)
+        v_words.append(gather("v_words1", tab_win1, list1, U32, "v_words1"))
+        w1_raw11 = load_weight("w1_11", w1, 1, 1, 11)
+        w1_q10 = quantise_weight("w1_10", w1_raw10, "vs", ("woven0", "woven1"), "w1_10_codes")
+        we1_raw = load_weight("we1", we, 0, 1, 24)
+        held = []
+        for c in range(CHUNKS):
+            add_pass(second[c], fp4_pass(1, 0), c, False, True)
+            held.append(hold(second[c], "held0%d" % c))
+        least = ringed("least", [P, 4 * S], F32, 1)
+        for c in range(CHUNKS):
+            add_pass(first[c], fp8_pass(w1_q10, v_words[1], v_plane[:, 1, :]), c, False, True)
+            smaller(first[c], held[c], span(least, c))
+        w1_q01 = quantise_weight("w1_01", w1_raw01, "s", ("woven2",), "held03")
+        h_halves = [damped(span(least, c, 2), damp, c, 2, "h0%d" % c) for c in range(0, CHUNKS, 2)]
+        for n, h in enumerate(h_halves):
+            quantise_h(h, 0, 2 * n, 2)
 
-        w1_q1.append(quantise_weight("w1_11", w1_raw11, "vs"))
-        held1 = [second_response(1, c) for c in range(CHUNKS)]
-        we1_q = quantise_weight("we1", we1_raw, "vv")
+        w1_q11 = quantise_weight("w1_11", w1_raw11, "vs", ("h00", "woven1"), "w1_11_codes")
+        held = []
+        for c in range(CHUNKS):
+            bank = new_bank()
+            for a in range(2):
+                add_pass(bank, fp4_pass(a, 1), c, a == 0, a == 1)
+            held.append(hold(bank, "held1%d" % c))
+        first = [new_bank() for c in range(CHUNKS)]
+        for a, q in enumerate((w1_q01, w1_q11)):
+            for c in range(CHUNKS):
+                add_pass(first[c], fp8_pass(q, v_words[a], v_plane[:, a, :]), c, a == 0, a == 1)
+        we1_q = quantise_weight("we1", we1_raw, "vs", ("h02", "woven0"), "we1_codes")
 
         wj_raw = {}
 
-        def load_wj(g, slot):
-            wj_raw[g] = ringed(slot, [P, 2, 4, 256], F32, 1)
+        def load_wj(g, place):
+            wj_raw[g] = placed("wj_raw%d" % g, [P, 2, 4, 256], F32, place)
             for b in range(2):
                 rows = wj[512 * b : 512 * (b + 1), 256 * g : 256 * (g + 1)].rearrange("(i t u) n -> u i t n", t=4, u=4)
                 for u in range(4):
@@ -245,57 +270,62 @@ def tile_list_etched_weld_contrast_kernel(
 
         pages = {}
 
-        def load_page(n, slot):
-            pages[n] = ringed(slot, [P, T2], F32, 1)
+        def load_page(n, place):
+            pages[n] = placed("page%d" % n, [P, T2], F32, place)
             nc.sync.dma_start(out=pages[n][:], in_=page1[P * n : P * (n + 1), :])
 
-        load_wj(0, "slot_c")
-        gain = ringed("half", [P, S], F32, 4)
+        load_wj(0, 1)
+        gain = ringed("woven2", [P, S], F32, 1)
         nc.sync.dma_start(out=gain[:], in_=wgo)
-        load_page(0, "slot_d")
-        load_page(1, "slot_a")
-        load_wj(1, "slot_b")
+        load_page(0, "slot_a")
+        load_page(1, 11)
+        load_wj(1, 24)
 
-        wj_q = {}
-
-        def quantise_wj(n, engine):
-            codes = kept("wj_codes%d" % n, [P, 2, P], U32)
-            scales = kept("wj_scales%d" % n, [P, 2, P], U8)
-            both = ringed("both", [P, 2, P, 4], BF16, 2)
-            src = wj_raw[n // 2][:, :, :, P * (n % 2) : P * (n % 2 + 1)]
-            weave(engine, both[:].rearrange("p b (i u) t -> p b i t u", u=4), src.rearrange("p b t (i u) -> p b i t u", u=4))
+        def quantise_wj(g, tag):
+            codes = kept("wj_codes%d" % g, [P, 2, 2 * P], U32)
+            scales = kept("wj_scales%d" % g, [P, 2, 2 * P], U8)
+            both = ringed(tag, [P, 2, 2 * P, 4], BF16, 1)
+            for b in range(2):
+                nc.scalar.copy(
+                    out=both[:, b].rearrange("p (i u) t -> p i t u", u=4), in_=wj_raw[g][:, b].rearrange("p t (i u) -> p i t u", u=4)
+                )
             nc.vector.quantize_mx(
                 out=codes[:].rearrange("p b m -> p (b m)").bitcast(FP8X4),
                 scales=scales[:].rearrange("p b m -> p (b m)"),
                 in_=both[:].rearrange("p b m t -> p (b m t)"),
             )
-            wj_q[n] = (codes, scales)
+            return codes, scales
 
-        def contrast(n, c, count):
-            cols = slice(C * c, C * (c + count))
-            bank = psum.tile([P, C * count], F32, name="bank", tag="bank")
-            codes, scales = wj_q[n]
+        def contrast(target, q, half, cols):
+            codes, scales = q
+            rows = slice(P * half, P * (half + 1))
             for b in range(2):
                 nc.tensor.matmul_mx(
-                    out=bank[:],
-                    lhsT=codes[:, b, :].bitcast(FP8X4),
-                    lhsT_scale=scales[:, b, :],
+                    out=target,
+                    lhsT=codes[:, b, rows].bitcast(FP8X4),
+                    lhsT_scale=scales[:, b, rows],
                     rhs=h_codes[b][:, cols].bitcast(FP8X4),
                     rhs_scale=h_scales[b][:, cols],
                     start=(b == 0),
                     stop=(b == 1),
                 )
-            y = ringed("y", [P, C * count], F32, 4)
-            nc.scalar.copy(out=y[:], in_=bank[:])
-            return y
 
         def put(y, n, c, count):
             cols = slice(C * c, C * (c + count))
             entries = list3[:, C // 16 * c : C // 16 * (c + count)]
-            nc.vector.tensor_tensor(out=pages[n][:].indirect(entries), in0=y[:], in1=gain[:, cols], op=ALU.mult)
+            nc.vector.tensor_tensor(out=pages[n][:].indirect(entries), in0=y, in1=gain[:, cols], op=ALU.mult)
+
+        def put_chunk(c, tag):
+            bank = psum.tile([P, 2, C], F32, name="bank", tag="bank")
+            for n in range(2):
+                contrast(bank[:, n, :], wj_low, n, slice(C * c, C * (c + 1)))
+            y = ringed(tag, [P, 2, C], F32, 1)
+            nc.scalar.copy(out=y[:], in_=bank[:])
+            for n in range(2):
+                put(y[:, n, :], n, c, 1)
 
         def finish_h(c):
-            quantise_h(damped(least1[c], span(damp, c)), 1, c)
+            quantise_h(damped(least1[c][:], damp, c, 1, "h1%d" % (c % 2)), 1, c)
 
         def store(n):
             nc.sync.dma_start(out=out[P * n : P * (n + 1), :], in_=pages[n][:])
@@ -306,31 +336,30 @@ def tile_list_etched_weld_contrast_kernel(
         take_root(size, root, 0)
         take_size(we1_q, size, 2)
         take_square(root, damp, 0)
-        least1 = [smaller(w1_q1, held1[c], c) for c in range(CHUNKS)]
-        quantise_wj(0, "v")
-        finish_h(0)
         take_root(size, root, 1)
         take_size(we1_q, size, 3)
         take_square(root, damp, 1)
-        y = contrast(0, 0, 1)
+        least1 = [ringed("least%d" % c, [P, 4 * C], F32, 1) for c in range(CHUNKS)]
+        for c in range(CHUNKS):
+            smaller(first[c], held[c], least1[c][:])
+        wj_low = quantise_wj(0, "both0")
+        load_page(2, 1)
+        load_page(3, "w1_11_codes")
+        finish_h(0)
         for c in range(1, CHUNKS):
             finish_h(c)
-            put(y, 0, c - 1, 1)
+            put_chunk(c - 1, "least%d" % c)
             if c + 1 < CHUNKS:
                 take_root(size, root, c + 1)
-            y = contrast(0, c, 1)
-            if c + 1 < CHUNKS:
                 take_square(root, damp, c + 1)
-        quantise_wj(1, "s")
-        load_page(2, "slot_c")
-        load_page(3, "w1_11_codes")
-        put(y, 0, CHUNKS - 1, 1)
-        store(0)
-        y = contrast(1, 0, 4)
-        for n in range(1, 4):
-            if n < 3:
-                quantise_wj(n + 1, "s")
-            put(y, n, 0, 4)
+        wj_high = quantise_wj(1, "both1")
+        put_chunk(CHUNKS - 1, "both1")
+        for n in range(2):
             store(n)
-            if n < 3:
-                y = contrast(n + 1, 0, 4)
+        for n in range(2, 4):
+            bank = psum.tile([P, S], F32, name="bank", tag="bank")
+            contrast(bank[:], wj_high, n - 2, slice(0, S))
+            y = ringed("y", [P, S], F32, 2)
+            nc.scalar.copy(out=y[:], in_=bank[:])
+            put(y[:], n, 0, CHUNKS)
+            store(n)

@@ -40,21 +40,19 @@ def tile_list_etched_weld_contrast_kernel(
         def placed(name, shape, dtype, place):
             if isinstance(place, str):
                 return ringed(place, shape, dtype, 1)
-            return lap.tile(shape, dtype, name=name, tag=name, offset=1024 * place, align_bytes=64)
+            return lap.tile(shape, dtype, name=name, tag=name, offset=int(1024 * place), align_bytes=64)
 
         list1 = kept("list1", [P, S // 16], U16)
         list2 = kept("list2", [P, S // 16], U16)
         list3 = kept("list3", [P, S // 16], U16)
-        tab_sc = [placed("tab_sc%d" % a, [P, T], U8, 8 + 2 * a) for a in range(2)]
-        tab2_sc = placed("tab2_sc", [P, T], U8, 24)
+        tab_sc = placed("tab_sc", [P, T], U8, 10)
+        tab2_sc = placed("tab2_sc", [P, T], U8, 28)
         tab2_rows = ringed("slot_c", [P, T // 4], I32, 1)
-        w2_sc_raw = kept("w2_sc_raw", [P, 2, H], U8)
+        w2_sc_raw = ringed("w2_sc_raw", [P, 2, H], U8, 1)
         v_plane = kept("v_plane", [P, 2, S], U8)
-        nc.vector.memset(tab2_sc[:].bitcast(I32), 0)
-        nc.gpsimd.memset(tab_sc[0][:].bitcast(I32), 0)
-        nc.vector.memset(tab_sc[1][:].bitcast(I32), 0)
-        for zeroed in (w2_sc_raw, v_plane):
-            nc.vector.memset(zeroed[:].rearrange("p a n -> p (a n)").bitcast(I32), 0)
+        nc.gpsimd.memset(w2_sc_raw[:].rearrange("p a n -> p (a n)").bitcast(I32), 0)
+        for zeroed in (tab_sc[:], tab2_sc[:], v_plane[:].rearrange("p a n -> p (a n)")):
+            nc.vector.memset(zeroed.bitcast(I32), 0)
 
         for d in range(4):
             nc.gpsimd.dma_start(
@@ -127,22 +125,19 @@ def tile_list_etched_weld_contrast_kernel(
             codes, scales = q
             return (lambda t: codes[:, P * t : P * (t + 1)].bitcast(FP8X4), lambda t: scales[:, P * t : P * (t + 1)], rhs, rhs_scale)
 
-        def damping_tiles():
-            return [ringed(tag, [P, 4 * S], F32, 1) for tag in ("size", "root", "damp")]
-
         def span(tile, c, count=1):
             return tile[:, 4 * C * c : 4 * C * (c + count)]
 
         def take_size(we_q, size, c):
             bank = new_bank()
             add_pass(bank, fp8_pass(we_q, v2_words, v2_plane), c, True, True)
-            nc.scalar.activation(out=woven(span(size, c)), in_=stepped(bank), func=ACT.Abs)
+            nc.scalar.activation(out=woven(size), in_=stepped(bank), func=ACT.Abs)
 
-        def take_root(size, root, c, count=1):
-            nc.scalar.activation(out=span(root, c, count), in_=span(size, c, count), func=ACT.Abs_reciprocal_sqrt, bias=1.0)
+        def take_root(size, root):
+            nc.scalar.activation(out=root, in_=size, func=ACT.Abs_reciprocal_sqrt, bias=1.0)
 
-        def take_square(root, damp, c, count=1):
-            nc.scalar.activation(out=span(damp, c, count), in_=span(root, c, count), func=ACT.Square)
+        def take_square(root, damp):
+            nc.scalar.activation(out=damp, in_=root, func=ACT.Square)
 
         def fp4_pass(a, b):
             return (
@@ -179,7 +174,7 @@ def tile_list_etched_weld_contrast_kernel(
         tab2_win = load_words("tab2_win", tab2_words[0], "slot_b")
         nc.sync.dma_start(list1[:], offs)
         for a in range(2):
-            nc.sync.dma_start(out=tab_sc[a][0:P:8, :].bitcast(I32), in_=tab_scales[a].bitcast(I32))
+            nc.sync.dma_start(out=tab_sc[a:P:8, :].bitcast(I32), in_=tab_scales[a].bitcast(I32))
         nc.sync.dma_start(list3[:], offs3)
 
         for d in range(4):
@@ -187,52 +182,54 @@ def tile_list_etched_weld_contrast_kernel(
         w2_raw = ringed("slot_c", [P, 2, 512], I32, 1)
         nc.sync.dma_start(out=w2_raw[:], in_=w2_words.rearrange("a p n -> p a n").bitcast(I32))
         v2_plane = gather("v2_plane", tab2_sc, list2, U8, "v2_plane")
-        tab_win0 = load_words("tab_win0", tab_words[0], 22)
+        tab_win0 = load_words("tab_win0", tab_words[0], 26)
         we0_q = quantise_weight("we0", we0_raw, "vs", ("woven0", "early"), "we0_codes")
         v2_words = gather("v2_words", tab2_win, list2, U32, "v2_words")
         w1_raw00 = load_weight("w1_00", w1, 0, 0, "slot_a")
-        v_sc = ringed("early", [P, 2, S], U8, 1)
-        for a in range(2):
-            nc.vector.tensor_copy(v_sc[:, a, :], tab_sc[a][:].indirect(list1[:]))
-        for d in range(4):
-            nc.sync.dma_start(
-                out=v_plane[32 * d : 32 * d + 4].rearrange("p a n -> p (a n)").bitcast(I32),
-                in_=v_sc[32 * d : 32 * (d + 1) : 8].rearrange("p a n -> p (a n)").bitcast(I32),
-            )
+        v_sc = gather("v_sc", tab_sc, list1, U8, "early")
+
+        def move_scales(a):
+            for d in range(4):
+                nc.sync.dma_start(
+                    out=v_plane[32 * d : 32 * d + 4, a, :].bitcast(I32), in_=v_sc[32 * d + a : 32 * (d + 1) : 8, :].bitcast(I32)
+                )
+
+        move_scales(0)
         tab_win1 = load_words("tab_win1", tab_words[1], 11)
+        move_scales(1)
 
-        size, root, damp = damping_tiles()
+        size, root, damp = [ringed(tag, [P, 4 * S], F32, 1) for tag in ("size", "root", "damp")]
         for c in range(CHUNKS):
-            take_size(we0_q, size, c)
+            take_size(we0_q, span(size, c), c)
         for c in range(0, CHUNKS, 2):
-            take_root(size, root, c, 2)
+            take_root(span(size, c, 2), span(root, c, 2))
         for c in range(0, CHUNKS, 2):
-            take_square(root, damp, c, 2)
+            take_square(span(root, c, 2), span(damp, c, 2))
 
-        w2_dealt = placed("w2_dealt", [P, 16, 2 * P], U8, 5)
+        w2_dealt = placed("w2_dealt", [P, 16, 2 * P], U8, 3)
         nc.vector.tensor_copy(
             out=w2_dealt[:].bitcast(I32).rearrange("p (g t) (i w) -> p g t i w", t=4, w=2),
             in_=w2_raw[:].rearrange("p a (b i t w) -> p (a b) t i w", b=2, t=4, w=2),
         )
-        w2_sc = ringed("slot_c", [P, 16, P], U8, 1)
+        v_words = [gather("v_words0", tab_win0, list1, U32, 9)]
+        w1_raw10 = load_weight("w1_10", w1, 1, 0, 28)
+        w1_q00 = quantise_weight("w1_00", w1_raw00, "v", (24,), "w1_00_codes")
+        w2_sc = placed("w2_sc", [P, 16, P], U8, 24)
         nc.vector.tensor_copy(
             out=w2_sc[:].bitcast(I32).rearrange("p (g t) i -> p g t i", t=4),
             in_=w2_sc_raw[:].bitcast(I32).rearrange("p a (b i t) -> p (a b) t i", b=2, t=4),
         )
-        v_words = [gather("v_words0", tab_win0, list1, U32, 9)]
-        w1_raw10 = load_weight("w1_10", w1, 1, 0, 24)
-        second = [new_bank() for c in range(CHUNKS)]
-        for c in range(CHUNKS):
-            add_pass(second[c], fp4_pass(0, 0), c, True, False)
-        w1_q00 = quantise_weight("w1_00", w1_raw00, "v", (20,), "w1_00_codes")
         w1_raw01 = load_weight("w1_01", w1, 0, 1, "slot_a")
+        second = [new_bank() for c in range(CHUNKS)]
         first = [new_bank() for c in range(CHUNKS)]
         for c in range(CHUNKS):
             add_pass(first[c], fp8_pass(w1_q00, v_words[0], v_plane[:, 0, :]), c, True, False)
-        v_words.append(gather("v_words1", tab_win1, list1, U32, "v_words1"))
-        w1_raw11 = load_weight("w1_11", w1, 1, 1, 11)
-        w1_q10 = quantise_weight("w1_10", w1_raw10, "vs", ("woven0", "woven1"), "w1_10_codes")
-        we1_raw = load_weight("we1", we, 0, 1, 24)
+        for c in range(CHUNKS):
+            add_pass(second[c], fp4_pass(0, 0), c, True, False)
+        v_words.append(gather("v_words1", tab_win1, list1, U32, "w2_sc_raw"))
+        w1_raw11 = load_weight("w1_11", w1, 1, 1, 15)
+        w1_q10 = quantise_weight("w1_10", w1_raw10, "v", (11,), "w1_10_codes")
+        we1_raw = load_weight("we1", we, 0, 1, 28)
         held = []
         for c in range(CHUNKS):
             add_pass(second[c], fp4_pass(1, 0), c, False, True)
@@ -241,7 +238,7 @@ def tile_list_etched_weld_contrast_kernel(
         for c in range(CHUNKS):
             add_pass(first[c], fp8_pass(w1_q10, v_words[1], v_plane[:, 1, :]), c, False, True)
             smaller(first[c], held[c], span(least, c))
-        w1_q01 = quantise_weight("w1_01", w1_raw01, "s", ("woven2",), "held03")
+        w1_q01 = quantise_weight("w1_01", w1_raw01, "s", ("held00",), "held03")
         h_halves = [damped(span(least, c, 2), damp, c, 2, "h0%d" % c) for c in range(0, CHUNKS, 2)]
         for n, h in enumerate(h_halves):
             quantise_h(h, 0, 2 * n, 2)
@@ -259,14 +256,13 @@ def tile_list_etched_weld_contrast_kernel(
                 add_pass(first[c], fp8_pass(q, v_words[a], v_plane[:, a, :]), c, a == 0, a == 1)
         we1_q = quantise_weight("we1", we1_raw, "vs", ("h02", "woven0"), "we1_codes")
 
-        wj_raw = {}
-
         def load_wj(g, place):
-            wj_raw[g] = placed("wj_raw%d" % g, [P, 2, 4, 256], F32, place)
+            raws = [placed("wj_raw%d%d" % (g, b), [P, 4, 256], F32, place + 4 * b) for b in range(2)]
             for b in range(2):
                 rows = wj[512 * b : 512 * (b + 1), 256 * g : 256 * (g + 1)].rearrange("(i t u) n -> u i t n", t=4, u=4)
                 for u in range(4):
-                    nc.sync.dma_start(out=wj_raw[g][u:P:4, b], in_=rows[u])
+                    nc.sync.dma_start(out=raws[b][u:P:4], in_=rows[u])
+            return raws
 
         pages = {}
 
@@ -274,26 +270,20 @@ def tile_list_etched_weld_contrast_kernel(
             pages[n] = placed("page%d" % n, [P, T2], F32, place)
             nc.sync.dma_start(out=pages[n][:], in_=page1[P * n : P * (n + 1), :])
 
-        load_wj(0, 1)
-        gain = ringed("woven2", [P, S], F32, 1)
+        wj_raw_low = load_wj(0, 1)
+        gain = ringed("held00", [P, S], F32, 1)
         nc.sync.dma_start(out=gain[:], in_=wgo)
         load_page(0, "slot_a")
-        load_page(1, 11)
-        load_wj(1, 24)
+        load_page(1, 15)
+        wj_raw_high = load_wj(1, 28)
 
-        def quantise_wj(g, tag):
-            codes = kept("wj_codes%d" % g, [P, 2, 2 * P], U32)
-            scales = kept("wj_scales%d" % g, [P, 2, 2 * P], U8)
-            both = ringed(tag, [P, 2, 2 * P, 4], BF16, 1)
+        def quantise_wj(name, raws, tags):
+            codes = kept(name + "_codes", [P, 2, 2 * P], U32)
+            scales = kept(name + "_scales", [P, 2, 2 * P], U8)
             for b in range(2):
-                nc.scalar.copy(
-                    out=both[:, b].rearrange("p (i u) t -> p i t u", u=4), in_=wj_raw[g][:, b].rearrange("p t (i u) -> p i t u", u=4)
-                )
-            nc.vector.quantize_mx(
-                out=codes[:].rearrange("p b m -> p (b m)").bitcast(FP8X4),
-                scales=scales[:].rearrange("p b m -> p (b m)"),
-                in_=both[:].rearrange("p b m t -> p (b m t)"),
-            )
+                part = ringed(tags[b], [P, 2 * P, 4], BF16, 1)
+                nc.scalar.copy(out=part[:].rearrange("p (i u) t -> p i t u", u=4), in_=raws[b][:].rearrange("p t (i u) -> p i t u", u=4))
+                nc.vector.quantize_mx(out=codes[:, b, :].bitcast(FP8X4), scales=scales[:, b, :], in_=part[:].rearrange("p m t -> p (m t)"))
             return codes, scales
 
         def contrast(target, q, half, cols):
@@ -315,11 +305,11 @@ def tile_list_etched_weld_contrast_kernel(
             entries = list3[:, C // 16 * c : C // 16 * (c + count)]
             nc.vector.tensor_tensor(out=pages[n][:].indirect(entries), in0=y, in1=gain[:, cols], op=ALU.mult)
 
-        def put_chunk(c, tag):
+        def put_chunk(c, place):
             bank = psum.tile([P, 2, C], F32, name="bank", tag="bank")
             for n in range(2):
                 contrast(bank[:, n, :], wj_low, n, slice(C * c, C * (c + 1)))
-            y = ringed(tag, [P, 2, C], F32, 1)
+            y = placed("y_chunk%d" % c, [P, 2, C], F32, place)
             nc.scalar.copy(out=y[:], in_=bank[:])
             for n in range(2):
                 put(y[:, n, :], n, c, 1)
@@ -330,30 +320,28 @@ def tile_list_etched_weld_contrast_kernel(
         def store(n):
             nc.sync.dma_start(out=out[P * n : P * (n + 1), :], in_=pages[n][:])
 
-        size, root, damp = damping_tiles()
-        take_size(we1_q, size, 0)
-        take_size(we1_q, size, 1)
-        take_root(size, root, 0)
-        take_size(we1_q, size, 2)
-        take_square(root, damp, 0)
-        take_root(size, root, 1)
-        take_size(we1_q, size, 3)
-        take_square(root, damp, 1)
-        least1 = [ringed("least%d" % c, [P, 4 * C], F32, 1) for c in range(CHUNKS)]
+        size, damp = [ringed(tag, [P, 4 * S], F32, 1) for tag in ("size", "damp")]
+        roots = [ringed("root%d" % c, [P, 4 * C], F32, 1) for c in range(CHUNKS)]
+        for c in range(CHUNKS):
+            take_size(we1_q, span(size, c), c)
+        for c in range(CHUNKS):
+            take_root(span(size, c), roots[c][:])
+            take_square(roots[c][:], span(damp, c))
+        least1 = [placed("least%d" % c, [P, 4 * C], F32, place) for c, place in enumerate(("least0", "least1", 26, 36))]
         for c in range(CHUNKS):
             smaller(first[c], held[c], least1[c][:])
-        wj_low = quantise_wj(0, "both0")
+        wj_low = quantise_wj("wj_low", wj_raw_low, ("low0", "low1"))
         load_page(2, 1)
         load_page(3, "w1_11_codes")
         finish_h(0)
-        for c in range(1, CHUNKS):
-            finish_h(c)
-            put_chunk(c - 1, "least%d" % c)
-            if c + 1 < CHUNKS:
-                take_root(size, root, c + 1)
-                take_square(root, damp, c + 1)
-        wj_high = quantise_wj(1, "both1")
-        put_chunk(CHUNKS - 1, "both1")
+        finish_h(1)
+        put_chunk(0, "least1")
+        wj_high = quantise_wj("wj_high", wj_raw_high, ("root2", "root3"))
+        finish_h(2)
+        put_chunk(1, 27.5)
+        finish_h(3)
+        put_chunk(2, 35.5)
+        put_chunk(3, "root3")
         for n in range(2):
             store(n)
         for n in range(2, 4):

from contextlib import ExitStack

import concourse.mybir as mybir

K, J, H, N, T, S, T2 = 1024, 512, 1024, 512, 2048, 512, 1024
FLOPS = 2 * S * (2 * K * H + J * H + H * N)

F32 = mybir.dt.float32
BF16 = mybir.dt.bfloat16
I32 = mybir.dt.int32
U32 = mybir.dt.uint32
U16 = mybir.dt.uint16
U8 = mybir.dt.uint8
FP8X4 = mybir.dt.float8_e4m3fn_x4
FP4X4 = mybir.dt.float4_e2m1fn_x4
ACT = mybir.ActivationFunctionType
ALU = mybir.AluOpType

P = 128
C = 128
CHUNKS = S // C


def tile_list_etched_weld_contrast_kernel(
    tc, tab_words, tab_scales, offs, tab2_words, tab2_scales, offs2, w1, w2_words, w2_scales, we, wj, page1, wgo, offs3, out
):
    nc = tc.nc
    with ExitStack() as ctx:
        keep = ctx.enter_context(tc.tile_pool(name="keep", bufs=1))
        ring = ctx.enter_context(tc.tile_pool(name="ring", bufs=1))
        lap = ctx.enter_context(tc.tile_pool(name="lap", bufs=1))
        psum = ctx.enter_context(tc.psum_pool(name="psum", bufs=8))

        def kept(name, shape, dtype):
            return keep.tile(shape, dtype, name=name, align_bytes=64)

        def ringed(tag, shape, dtype, bufs):
            return ring.tile(shape, dtype, name=tag, tag=tag, bufs=bufs, align_bytes=64)

        def placed(name, shape, dtype, place):
            if isinstance(place, str):
                return ringed(place, shape, dtype, 1)
            return lap.tile(shape, dtype, name=name, tag=name, offset=int(1024 * place), align_bytes=64)

        list1 = kept("list1", [P, S // 16], U16)
        list2 = kept("list2", [P, S // 16], U16)
        list3 = kept("list3", [P, S // 16], U16)
        tab_sc = placed("tab_sc", [P, T], U8, 10)
        tab2_sc = placed("tab2_sc", [P, T], U8, 28)
        tab2_rows = ringed("slot_c", [P, T // 4], I32, 1)
        w2_sc_raw = ringed("w2_sc_raw", [P, 2, H], U8, 1)
        v_plane = kept("v_plane", [P, 2, S], U8)
        nc.gpsimd.memset(w2_sc_raw[:].rearrange("p a n -> p (a n)").bitcast(I32), 0)
        for zeroed in (tab_sc[:], tab2_sc[:], v_plane[:].rearrange("p a n -> p (a n)")):
            nc.vector.memset(zeroed.bitcast(I32), 0)

        for d in range(4):
            nc.gpsimd.dma_start(
                out=w2_sc_raw[32 * d : 32 * d + 4].bitcast(I32),
                in_=w2_scales[:, 4 * d : 4 * d + 4, :].rearrange("a q n -> q a n").bitcast(I32),
            )

        def load_weight(name, w, a, b, place):
            raw = placed(name, [P, 4, 512], F32, place)
            nc.sync.dma_start(out=raw[:], in_=w[512 * a : 512 * (a + 1), 512 * b : 512 * (b + 1)].rearrange("(p j) c -> p j c", j=4))
            return raw

        def load_words(name, words, place):
            win = placed(name, [P, T], U32, place)
            nc.sync.dma_start(out=win[:].bitcast(I32), in_=words.rearrange("p t i -> p (t i)").bitcast(I32))
            return win

        def gather(name, win, lst, dtype, place):
            got = placed(name, [P, S], dtype, place)
            nc.vector.tensor_copy(got[:], win[:].indirect(lst[:]))
            return got

        def weave(engine, dst, src):
            if engine == "v":
                nc.vector.tensor_copy(out=dst, in_=src)
            else:
                nc.scalar.copy(out=dst, in_=src)

        def quantise_weight(name, raw, engines, places, codes_place):
            codes = placed(name + "_codes", [P, 512], U32, codes_place)
            scales = kept(name + "_scales", [P, 512], U8)
            src = raw[:].rearrange("p j (i t u) -> p t i j u", t=4, u=4)
            share = 4 // len(engines)
            parts = []
            for h, engine in enumerate(engines):
                part = placed(name + "_woven%d" % h, [P, share, P, 4], BF16, places[h])
                weave(engine, part[:].rearrange("p t (i u) j -> p t i j u", u=4), src[:, share * h : share * (h + 1)])
                parts.append(part)
            for h, part in enumerate(parts):
                cols = slice(P * share * h, P * share * (h + 1))
                nc.vector.quantize_mx(
                    out=codes[:, cols].bitcast(FP8X4), scales=scales[:, cols], in_=part[:].rearrange("p t m j -> p (t m j)")
                )
            return codes, scales

        def new_bank():
            return psum.tile([P, 4, C], F32, name="bank", tag="bank")

        def add_pass(bank, operands, c, first, last):
            lhs, lhs_scale, rhs, rhs_scale = operands
            cols = slice(C * c, C * (c + 1))
            for t in range(4):
                nc.tensor.matmul_mx(
                    out=bank[:, t, :],
                    lhsT=lhs(t),
                    lhsT_scale=lhs_scale(t),
                    rhs=rhs[:, cols].bitcast(FP8X4),
                    rhs_scale=rhs_scale[:, cols],
                    start=(first and t == 0),
                    stop=(last and t == 3),
                )

        def stepped(bank):
            return bank[:].rearrange("p t j -> p j t")

        def woven(ap):
            return ap.rearrange("p (j t) -> p j t", t=4)

        def fp8_pass(q, rhs, rhs_scale):
            codes, scales = q
            return (lambda t: codes[:, P * t : P * (t + 1)].bitcast(FP8X4), lambda t: scales[:, P * t : P * (t + 1)], rhs, rhs_scale)

        def span(tile, c, count=1):
            return tile[:, 4 * C * c : 4 * C * (c + count)]

        def take_size(we_q, size, c):
            bank = new_bank()
            add_pass(bank, fp8_pass(we_q, v2_words, v2_plane), c, True, True)
            nc.scalar.activation(out=woven(size), in_=stepped(bank), func=ACT.Abs)

        def take_root(size, root):
            nc.scalar.activation(out=root, in_=size, func=ACT.Abs_reciprocal_sqrt, bias=1.0)

        def take_square(root, damp):
            nc.scalar.activation(out=damp, in_=root, func=ACT.Square)

        def fp4_pass(a, b):
            return (
                lambda t: w2_dealt[:, 8 * a + 4 * b + t, :].bitcast(FP4X4),
                lambda t: w2_sc[:, 8 * a + 4 * b + t, :],
                v_words[a],
                v_plane[:, a, :],
            )

        def hold(bank, tag):
            held = ringed(tag, [P, 4 * C], F32, 1)
            nc.scalar.copy(out=woven(held[:]), in_=stepped(bank))
            return held

        def smaller(bank, held, least):
            nc.vector.tensor_tensor(out=woven(least), in0=stepped(bank), in1=woven(held[:]), op=ALU.min)

        h_codes = [kept("h_codes%d" % b, [P, S], U32) for b in range(2)]
        h_scales = [kept("h_scales%d" % b, [P, S], U8) for b in range(2)]

        def damped(least, damp, c, count, tag):
            h = ringed(tag, [P, 4 * C * count], BF16, 1)
            nc.vector.tensor_tensor(out=h[:], in0=least, in1=span(damp, c, count), op=ALU.mult)
            return h

        def quantise_h(h, b, c, count=1):
            cols = slice(C * c, C * (c + count))
            nc.vector.quantize_mx(out=h_codes[b][:, cols].bitcast(FP8X4), scales=h_scales[b][:, cols], in_=h[:])

        nc.sync.dma_start(list2[:], offs2)
        for d in range(4):
            nc.sync.dma_start(out=tab2_rows[32 * d : 32 * d + 4, :], in_=tab2_scales[0, 4 * d : 4 * d + 4, :].bitcast(I32))
        we0_raw = load_weight("we0", we, 0, 0, "slot_a")
        tab2_win = load_words("tab2_win", tab2_words[0], "slot_b")
        nc.sync.dma_start(list1[:], offs)
        for a in range(2):
            nc.sync.dma_start(out=tab_sc[a:P:8, :].bitcast(I32), in_=tab_scales[a].bitcast(I32))
        nc.sync.dma_start(list3[:], offs3)

        for d in range(4):
            nc.vector.tensor_copy(out=tab2_sc[32 * d : 32 * d + 4, :].bitcast(I32), in_=tab2_rows[32 * d : 32 * d + 4, :])
        w2_raw = ringed("slot_c", [P, 2, 512], I32, 1)
        nc.sync.dma_start(out=w2_raw[:], in_=w2_words.rearrange("a p n -> p a n").bitcast(I32))
        v2_plane = gather("v2_plane", tab2_sc, list2, U8, "v2_plane")
        tab_win0 = load_words("tab_win0", tab_words[0], 26)
        we0_q = quantise_weight("we0", we0_raw, "vs", ("woven0", "early"), "we0_codes")
        v2_words = gather("v2_words", tab2_win, list2, U32, "v2_words")
        w1_raw00 = load_weight("w1_00", w1, 0, 0, "slot_a")
        v_sc = gather("v_sc", tab_sc, list1, U8, "early")

        def move_scales(a):
            for d in range(4):
                nc.sync.dma_start(
                    out=v_plane[32 * d : 32 * d + 4, a, :].bitcast(I32), in_=v_sc[32 * d + a : 32 * (d + 1) : 8, :].bitcast(I32)
                )

        move_scales(0)
        tab_win1 = load_words("tab_win1", tab_words[1], 11)
        move_scales(1)

        size, root, damp = [ringed(tag, [P, 4 * S], F32, 1) for tag in ("size", "root", "damp")]
        for c in range(CHUNKS):
            take_size(we0_q, span(size, c), c)
        for c in range(0, CHUNKS, 2):
            take_root(span(size, c, 2), span(root, c, 2))
        for c in range(0, CHUNKS, 2):
            take_square(span(root, c, 2), span(damp, c, 2))

        w2_dealt = placed("w2_dealt", [P, 16, 2 * P], U8, 3)
        nc.vector.tensor_copy(
            out=w2_dealt[:].bitcast(I32).rearrange("p (g t) (i w) -> p g t i w", t=4, w=2),
            in_=w2_raw[:].rearrange("p a (b i t w) -> p (a b) t i w", b=2, t=4, w=2),
        )
        v_words = [gather("v_words0", tab_win0, list1, U32, 9)]
        w1_raw10 = load_weight("w1_10", w1, 1, 0, 28)
        w1_q00 = quantise_weight("w1_00", w1_raw00, "v", (24,), "w1_00_codes")
        w2_sc = placed("w2_sc", [P, 16, P], U8, 24)
        nc.vector.tensor_copy(
            out=w2_sc[:].bitcast(I32).rearrange("p (g t) i -> p g t i", t=4),
            in_=w2_sc_raw[:].bitcast(I32).rearrange("p a (b i t) -> p (a b) t i", b=2, t=4),
        )
        w1_raw01 = load_weight("w1_01", w1, 0, 1, "slot_a")
        second = [new_bank() for c in range(CHUNKS)]
        first = [new_bank() for c in range(CHUNKS)]
        for c in range(CHUNKS):
            add_pass(first[c], fp8_pass(w1_q00, v_words[0], v_plane[:, 0, :]), c, True, False)
        for c in range(CHUNKS):
            add_pass(second[c], fp4_pass(0, 0), c, True, False)
        v_words.append(gather("v_words1", tab_win1, list1, U32, "w2_sc_raw"))
        w1_raw11 = load_weight("w1_11", w1, 1, 1, 15)
        w1_q10 = quantise_weight("w1_10", w1_raw10, "v", (11,), "w1_10_codes")
        we1_raw = load_weight("we1", we, 0, 1, 28)
        held = []
        for c in range(CHUNKS):
            add_pass(second[c], fp4_pass(1, 0), c, False, True)
            held.append(hold(second[c], "held0%d" % c))
        least = ringed("least", [P, 4 * S], F32, 1)
        for c in range(CHUNKS):
            add_pass(first[c], fp8_pass(w1_q10, v_words[1], v_plane[:, 1, :]), c, False, True)
            smaller(first[c], held[c], span(least, c))
        w1_q01 = quantise_weight("w1_01", w1_raw01, "s", ("held00",), "held03")
        h_halves = [damped(span(least, c, 2), damp, c, 2, "h0%d" % c) for c in range(0, CHUNKS, 2)]
        for n, h in enumerate(h_halves):
            quantise_h(h, 0, 2 * n, 2)

        w1_q11 = quantise_weight("w1_11", w1_raw11, "vs", ("h00", "woven1"), "w1_11_codes")
        held = []
        for c in range(CHUNKS):
            bank = new_bank()
            for a in range(2):
                add_pass(bank, fp4_pass(a, 1), c, a == 0, a == 1)
            held.append(hold(bank, "held1%d" % c))
        first = [new_bank() for c in range(CHUNKS)]
        for a, q in enumerate((w1_q01, w1_q11)):
            for c in range(CHUNKS):
                add_pass(first[c], fp8_pass(q, v_words[a], v_plane[:, a, :]), c, a == 0, a == 1)
        we1_q = quantise_weight("we1", we1_raw, "vs", ("h02", "woven0"), "we1_codes")

        def load_wj(g, place):
            raws = [placed("wj_raw%d%d" % (g, b), [P, 4, 256], F32, place + 4 * b) for b in range(2)]
            for b in range(2):
                rows = wj[512 * b : 512 * (b + 1), 256 * g : 256 * (g + 1)].rearrange("(i t u) n -> u i t n", t=4, u=4)
                for u in range(4):
                    nc.sync.dma_start(out=raws[b][u:P:4], in_=rows[u])
            return raws

        pages = {}

        def load_page(n, place):
            pages[n] = placed("page%d" % n, [P, T2], F32, place)
            nc.sync.dma_start(out=pages[n][:], in_=page1[P * n : P * (n + 1), :])

        wj_raw_low = load_wj(0, 1)
        gain = ringed("held00", [P, S], F32, 1)
        nc.sync.dma_start(out=gain[:], in_=wgo)
        load_page(0, "slot_a")
        load_page(1, 15)
        wj_raw_high = load_wj(1, 28)

        def quantise_wj(name, raws, tags):
            codes = kept(name + "_codes", [P, 2, 2 * P], U32)
            scales = kept(name + "_scales", [P, 2, 2 * P], U8)
            for b in range(2):
                part = ringed(tags[b], [P, 2 * P, 4], BF16, 1)
                nc.scalar.copy(out=part[:].rearrange("p (i u) t -> p i t u", u=4), in_=raws[b][:].rearrange("p t (i u) -> p i t u", u=4))
                nc.vector.quantize_mx(out=codes[:, b, :].bitcast(FP8X4), scales=scales[:, b, :], in_=part[:].rearrange("p m t -> p (m t)"))
            return codes, scales

        def contrast(target, q, half, cols):
            codes, scales = q
            rows = slice(P * half, P * (half + 1))
            for b in range(2):
                nc.tensor.matmul_mx(
                    out=target,
                    lhsT=codes[:, b, rows].bitcast(FP8X4),
                    lhsT_scale=scales[:, b, rows],
                    rhs=h_codes[b][:, cols].bitcast(FP8X4),
                    rhs_scale=h_scales[b][:, cols],
                    start=(b == 0),
                    stop=(b == 1),
                )

        def put(y, n, c, count):
            cols = slice(C * c, C * (c + count))
            entries = list3[:, C // 16 * c : C // 16 * (c + count)]
            nc.vector.tensor_tensor(out=pages[n][:].indirect(entries), in0=y, in1=gain[:, cols], op=ALU.mult)

        def put_chunk(c, place):
            bank = psum.tile([P, 2, C], F32, name="bank", tag="bank")
            for n in range(2):
                contrast(bank[:, n, :], wj_low, n, slice(C * c, C * (c + 1)))
            y = placed("y_chunk%d" % c, [P, 2, C], F32, place)
            nc.scalar.copy(out=y[:], in_=bank[:])
            for n in range(2):
                put(y[:, n, :], n, c, 1)

        def finish_h(c):
            quantise_h(damped(least1[c][:], damp, c, 1, "h1%d" % (c % 2)), 1, c)

        def store(n):
            nc.sync.dma_start(out=out[P * n : P * (n + 1), :], in_=pages[n][:])

        size, damp = [ringed(tag, [P, 4 * S], F32, 1) for tag in ("size", "damp")]
        roots = [ringed("root%d" % c, [P, 4 * C], F32, 1) for c in range(CHUNKS)]
        for c in range(CHUNKS):
            take_size(we1_q, span(size, c), c)
        for c in range(CHUNKS):
            take_root(span(size, c), roots[c][:])
            take_square(roots[c][:], span(damp, c))
        least1 = [placed("least%d" % c, [P, 4 * C], F32, place) for c, place in enumerate(("least0", "least1", 26, 36))]
        for c in range(CHUNKS):
            smaller(first[c], held[c], least1[c][:])
        wj_low = quantise_wj("wj_low", wj_raw_low, ("low0", "low1"))
        load_page(2, 1)
        load_page(3, "w1_11_codes")
        finish_h(0)
        finish_h(1)
        put_chunk(0, "least1")
        wj_high = quantise_wj("wj_high", wj_raw_high, ("root2", "root3"))
        finish_h(2)
        put_chunk(1, 27.5)
        finish_h(3)
        put_chunk(2, 35.5)
        put_chunk(3, "root3")
        for n in range(2):
            store(n)
        for n in range(2, 4):
            bank = psum.tile([P, S], F32, name="bank", tag="bank")
            contrast(bank[:], wj_high, n - 2, slice(0, S))
            y = ringed("y", [P, S], F32, 2)
            nc.scalar.copy(out=y[:], in_=bank[:])
            put(y[:], n, 0, CHUNKS)
            store(n)
